import numpy as np
import ml_dtypes


def mxq(x, axis, fmt="e4m3"):
    dtype, down = {"e4m3": (ml_dtypes.float8_e4m3fn, 7), "e5m2": (ml_dtypes.float8_e5m2, 14)}[fmt]
    v = np.moveaxis(np.asarray(x, np.float32).astype(ml_dtypes.bfloat16).astype(np.float64), axis, -1)
    blocks = v.reshape(v.shape[:-1] + (-1, 32))
    amax = np.abs(blocks).max(-1, keepdims=True)
    byte = np.maximum(np.where(amax > 0, np.frexp(amax)[1] - 1 + 127, 0) - down, 1)
    scale = np.exp2(byte - 127.0)
    codes = (blocks / scale).astype(np.float32).astype(dtype).astype(np.float64)
    return np.moveaxis((codes * scale).reshape(v.shape), -1, axis)


WIDE = False


def mx_kscale(k, group=512):
    if not WIDE:
        return np.ones(k)
    levels = np.array([10, -10, 5, -5, 0])
    if group != 512:
        return np.exp2(np.random.permutation(np.resize(levels, k // group))).repeat(group)
    if k % 512:
        return np.exp2(np.random.permutation(np.resize(levels, k // 32))).repeat(32)
    a = np.empty((k // 512, 16))
    for p in range(k // 512):
        a[p, :8] = np.random.permutation(np.resize(levels, 8))
        for g in range(8):
            far = levels[np.abs(levels - a[p, g]) >= 10]
            a[p, g + 8] = far[np.random.randint(len(far))]
    return np.exp2(a.ravel()).repeat(32)


def f64(x):
    return np.asarray(x).astype(np.float64)


G, D, K, M, N = 2, 256, 1024, 256, 512


def setup_inputs():
    n = np.random.standard_normal
    s = mx_kscale(D, 0)[:, None]
    u = mx_kscale(K)[:, None]
    return {
        "x": (n((G, D, N)) * s).astype(np.float32),
        "w1": (n((G, D, K)) / np.sqrt(D) / s).astype(np.float32),
        "hs": (np.random.uniform(0.5, 2.0, (G, K, 1)) * u).astype(np.float32),
        "w2": (n((G, K, M)) / np.sqrt(K) / u).astype(np.float32),
        "b": (0.5 * n((G, K, 1))).astype(np.float32),
        "r": n((G, M, N)).astype(np.float32),
    }


def reference(x, w1, hs, w2, b, r):
    xq = mxq(f64(x), 1, "e4m3")
    h = mxq(f64(w1), 1, "e4m3").transpose(0, 2, 1) @ xq
    h = h + f64(b)
    h = (np.square(np.maximum(h, 0.0))) * f64(hs)
    y = mxq(f64(w2), 1, "e4m3").transpose(0, 2, 1) @ mxq(h, 1, "e4m3")
    y = y + f64(r)
    return y

@@ -1,0 +1,263 @@
+from contextlib import ExitStack
+
+import concourse.mybir as mybir
+
+G, D, K, M, N = 2, 256, 1024, 256, 512
+FLOPS = 2 * G * D * K * N + 2 * G * K * M * N
+
+F32 = mybir.dt.float32
+BF16 = mybir.dt.bfloat16
+U32 = mybir.dt.uint32
+U8 = mybir.dt.uint8
+FP8X4 = mybir.dt.float8_e4m3fn_x4
+ALU = mybir.AluOpType
+ACT = mybir.ActivationFunctionType
+
+P = 128
+ROWS = 64
+NH = 256
+NC = 128
+TINY = 2.0 ** -110
+UNITS = [(0, 0, 0),(0, 1, 0),(1, 0, 0),(1, 1, 0),(0, 0, 1),(0, 1, 1),(1, 0, 1),(1, 1, 1)]
+
+
+def tile_rows_gmlp_relu2_bias_res_kernel(tc, x, w1, hs, w2, b, r, out):
+    nc = tc.nc
+    with ExitStack() as ctx:
+        sb = ctx.enter_context(tc.tile_pool(name="sb", bufs=1))
+        ps = ctx.enter_context(tc.psum_pool(name="ps", bufs=1))
+
+        def tiles(name, count, shape, dtype):
+            return [sb.tile(shape, dtype, name="%s%d" % (name, i), align_bytes=64) for i in range(count)]
+
+        x_raw = tiles("x_raw", 2, [P, 4, NH], F32)
+        x_bf = tiles("x_bf", 2, [P, NH, 4], BF16)
+        x_q = tiles("x_q", 2, [P, NH], U32)
+        x_s = tiles("x_s", 2, [P, NH], U8)
+        w1_raw = tiles("w1_raw", 4, [P, 4, 256], F32)
+        w1_bf = tiles("w1_bf", 2, [P, 4, P, 4], BF16)
+        w1_q = tiles("w1_q", 2, [P, 512], U32)
+        w1_s = tiles("w1_s", 2, [P, 512], U8)
+        w2_raw = tiles("w2_raw", 4, [P, 4, M], F32)
+        w2_bf = tiles("w2_bf", 2, [P, 2, M, 4], BF16)
+        w2_q = tiles("w2_q", 2, [P, 2 * M], U32)
+        w2_s = tiles("w2_s", 2, [P, 2 * M], U8)
+        r_sb = tiles("r_sb", 2, [P, 4, NH], F32)
+        t_sb = tiles("t_sb", 8, [P, 4, NH], F32)
+        h_bf = tiles("h_bf", 8, [P, NH, 4], BF16)
+        h_q = tiles("h_q", 8, [P, NH], U32)
+        h_s = tiles("h_s", 8, [P, NH], U8)
+        y_sb = tiles("y_sb", 5, [P, 2, NH], F32)
+        hs_sb, b_sb, mag, half, inv, quo, root, rootb, two, sgn = tiles("small", 10, [P, 4, 8], F32)
+        warm = tiles("warm", 2, [P, 1], F32)
+        z_ps = [[ps.tile([P, 2, NH], F32, name="z%d%d" % (g, i)) for i in range(2)] for g in range(G)]
+        y_ps = [ps.tile([P, 2, NH], F32, name="y%d" % i) for i in range(4)]
+
+        def live(t):
+            return t[:, :, 0:4]
+
+        def quantize(codes, scales, values):
+            nc.vector.quantize_mx(out=codes.bitcast(FP8X4), scales=scales, in_=values)
+
+        def rows4(t, lo, hi):
+            return t[:, :, lo:hi].rearrange("p j (c i) -> p c j i", i=4)
+
+        def words(t, lo, hi):
+            return t[:, lo:hi, :].rearrange("p (c i) j -> p c j i", i=4)
+
+        def copy(eng, o, i):
+            if eng == "A":
+                nc.scalar.copy(out=o, in_=i)
+            else:
+                nc.vector.tensor_copy(out=o, in_=i)
+
+        xv = x.rearrange("g (p j) n -> (g p) j n", j=4)
+        w1v = w1.rearrange("g (p j) k -> (g p) j k", j=4)
+
+        def load_x(h):
+            nc.sync.dma_start(out=x_raw[h][:], in_=xv[:, :, h * NH:(h + 1) * NH])
+
+        def load_w1(a):
+            nc.sync.dma_start(out=w1_raw[a][:], in_=w1v[:, :, a * 256:(a + 1) * 256])
+
+        def load_w2(g, c):
+            nc.sync.dma_start(out=w2_raw[2 * g + c][:], in_=w2[g, c * 512:(c + 1) * 512, :].rearrange("(p j) m -> p j m", j=4))
+
+        def load_r(h):
+            nc.sync.dma_start(out=r_sb[h][:], in_=r[:, :, h * NH:(h + 1) * NH].rearrange("g (t p) n -> p (g t) n", p=P))
+
+        def i_x(eng, h, lo, hi):
+            copy(eng, words(x_bf[h], lo, hi), rows4(x_raw[h], lo, hi))
+
+        def q_x(h, lo, hi):
+            quantize(x_q[h][:, lo:hi], x_s[h][:, lo:hi], x_bf[h][:, lo:hi, :].rearrange("p n j -> p (n j)"))
+
+        def i_w1(eng, a, lo, hi):
+            c, base = a // 2, (a % 2) * 64
+            copy(eng, w1_bf[c][:, :, base + lo:base + hi, :].rearrange("p t m j -> p m j t"),
+                 w1_raw[a][:, :, 4 * lo:4 * hi].rearrange("p j (m t) -> p m j t", t=4))
+
+        def q_w1(c, t0, t1):
+            quantize(w1_q[c][:, t0 * P:t1 * P], w1_s[c][:, t0 * P:t1 * P],
+                     w1_bf[c][:, t0:t1].rearrange("p t m j -> p (t m j)"))
+
+        def i_w2(g, c):
+            sign = sgn[:, 2 * g + c, 0:4].unsqueeze(1).unsqueeze(3).to_broadcast([P, M // 4, 4, 4])
+            nc.vector.tensor_tensor(out=words(w2_bf[g][:, c], 0, M), in0=rows4(w2_raw[2 * g + c], 0, M), in1=sign, op=ALU.mult)
+
+        def q_w2(g):
+            quantize(w2_q[g][:], w2_s[g][:], w2_bf[g][:].rearrange("p c m j -> p (c m j)"))
+
+        def mm1(u, i):
+            c, g, h = UNITS[u]
+            rows = slice(g * ROWS, (g + 1) * ROWS)
+            for q in range(2):
+                xc = slice(q * NC, (q + 1) * NC)
+                for tt in range(2):
+                    wc = slice((2 * i + tt) * P, (2 * i + tt + 1) * P)
+                    nc.tensor.matmul_mx(out=z_ps[g][i][:, tt, xc], lhsT=w1_q[c][rows, wc].bitcast(FP8X4), lhsT_scale=w1_s[c][rows, wc],
+                                        rhs=x_q[h][rows, xc].bitcast(FP8X4), rhs_scale=x_s[h][rows, xc], start=True, stop=True)
+
+        def s1(u, i):
+            c, g, h = UNITS[u]
+            for tt in range(2):
+                t = 2 * i + tt
+                nc.scalar.activation(out=t_sb[u][:, t, :], in_=z_ps[g][i][:, tt, :], func=ACT.Relu,
+                                     bias=rootb[:, 2 * g + c, t:t + 1], scale=root[:, 2 * g + c, t:t + 1])
+
+        def s2(eng, u, lo, hi):
+            src = rows4(t_sb[u], lo, hi)
+            if eng == "A":
+                nc.scalar.activation(out=words(h_bf[u], lo, hi), in_=src, func=ACT.Square)
+            else:
+                nc.vector.tensor_tensor(out=words(h_bf[u], lo, hi), in0=src, in1=src, op=ALU.mult)
+
+        def q_h(u, lo, hi):
+            quantize(h_q[u][:, lo:hi], h_s[u][:, lo:hi], h_bf[u][:, lo:hi, :].rearrange("p n j -> p (n j)"))
+
+        def mm2(u, bank, lo, hi):
+            g, h = UNITS[u][1:]
+            for n0 in range(lo, hi, NC):
+                xc = slice(n0, n0 + NC)
+                for mt in range(2):
+                    for c in range(2):
+                        hu = UNITS.index((c, g, h))
+                        wc = slice(c * M + mt * P, c * M + (mt + 1) * P)
+                        nc.tensor.matmul_mx(out=y_ps[bank][:, mt, xc], lhsT=w2_q[g][:, wc].bitcast(FP8X4), lhsT_scale=w2_s[g][:, wc],
+                                            rhs=h_q[hu][:, xc].bitcast(FP8X4), rhs_scale=h_s[hu][:, xc], start=(c == 0), stop=(c == 1))
+
+        def fin(u, bank, slot, lo, hi):
+            c, g, h = UNITS[u]
+            cols = slice(h * NH + lo, h * NH + hi)
+            nc.vector.tensor_tensor(out=y_sb[slot][:, :, lo:hi], in0=y_ps[bank][:, :, lo:hi], in1=r_sb[h][:, 2 * g:2 * g + 2, lo:hi], op=ALU.add)
+            nc.sync.dma_start(out=out[g, :, cols].rearrange("(t p) n -> p t n", p=P), in_=y_sb[slot][:, :, lo:hi])
+
+        with tc.manual_schedule():
+            nc.scalar.dma_start(out=live(hs_sb), in_=hs.rearrange("g (c p j) o -> p (g c) (j o)", p=P, j=4))
+            nc.scalar.dma_start(out=live(b_sb), in_=b.rearrange("g (c p j) o -> p (g c) (j o)", p=P, j=4))
+            load_w1(0)
+            load_w1(1)
+            load_x(0)
+            load_w1(2)
+            load_w1(3)
+            load_w2(0, 0)
+            load_w2(0, 1)
+            load_x(1)
+            load_w2(1, 0)
+            load_w2(1, 1)
+            load_r(0)
+            load_r(1)
+            nc.vector.memset(warm[0][:], 1.0)
+            nc.scalar.activation(out=warm[1][:], in_=warm[0][:], func=ACT.Sqrt)
+            nc.vector.scalar_tensor_tensor(out=live(mag), in0=live(hs_sb), scalar=-1.0, in1=live(hs_sb), op0=ALU.mult, op1=ALU.max)
+            nc.vector.tensor_scalar(out=live(two), in0=live(hs_sb), scalar1=0.0, scalar2=2.0, op0=ALU.is_ge, op1=ALU.mult)
+            nc.scalar.activation(out=live(half), in_=live(mag), func=ACT.Sqrt, scale=0.25, bias=TINY)
+            nc.vector.tensor_scalar(out=live(sgn), in0=live(two), scalar1=-1.0, scalar2=None, op0=ALU.add)
+            nc.vector.reciprocal(out=live(inv), in_=live(half))
+            i_w1("V", 0, 0, 40)
+            i_w1("A", 0, 40, 64)
+            nc.vector.scalar_tensor_tensor(out=live(quo), in0=live(mag), scalar=0.25, in1=live(inv), op0=ALU.mult, op1=ALU.mult)
+            i_w1("V", 1, 0, 40)
+            i_w1("A", 1, 40, 64)
+            nc.vector.tensor_tensor(out=live(root), in0=live(quo), in1=live(half), op=ALU.add)
+            q_w1(0, 0, 2)
+            nc.vector.tensor_tensor(out=live(rootb), in0=live(root), in1=live(b_sb), op=ALU.mult)
+            i_x("V", 0, 0, 128)
+            i_x("A", 0, 128, 256)
+            q_w1(0, 2, 4)
+            q_x(0, 0, 128)
+            q_x(0, 128, 256)
+            mm1(0, 0)
+            mm1(0, 1)
+            mm1(1, 0)
+            mm1(1, 1)
+            i_w1("V", 2, 0, 64)
+            s1(0, 0)
+            s1(0, 1)
+            i_w1("V", 3, 0, 64)
+            s1(1, 0)
+            s1(1, 1)
+            s2("V", 0, 0, 128)
+            q_w1(1, 0, 4)
+            mm1(2, 0)
+            mm1(2, 1)
+            mm1(3, 0)
+            mm1(3, 1)
+            i_w2(0, 0)
+            s2("A", 0, 128, 256)
+            s1(2, 0)
+            s1(2, 1)
+            i_w2(0, 1)
+            s1(3, 0)
+            s1(3, 1)
+            i_x("V", 1, 0, 256)
+            q_h(0, 0, 256)
+            q_x(1, 0, 256)
+            mm1(4, 0)
+            mm1(4, 1)
+            mm1(5, 0)
+            mm1(5, 1)
+            q_w2(0)
+            s2("A", 2, 0, 256)
+            i_w2(1, 0)
+            s2("A", 3, 0, 128)
+            q_h(2, 0, 256)
+            mm2(2, 0, 0, 256)
+            s1(4, 0)
+            s1(4, 1)
+            mm1(6, 0)
+            mm1(6, 1)
+            i_w2(1, 1)
+            s2("V", 1, 0, 256)
+            s1(5, 0)
+            s1(5, 1)
+            mm1(7, 0)
+            mm1(7, 1)
+            q_w2(1)
+            s2("V", 3, 128, 256)
+            q_h(1, 0, 256)
+            s1(6, 0)
+            s1(6, 1)
+            q_h(3, 0, 256)
+            mm2(3, 1, 0, 256)
+            s2("A", 4, 0, 128)
+            s2("V", 4, 128, 256)
+            fin(2, 0, 0, 0, 256)
+            s2("A", 6, 0, 256)
+            q_h(4, 0, 256)
+            s2("V", 5, 0, 256)
+            s1(7, 0)
+            s1(7, 1)
+            q_h(6, 0, 256)
+            mm2(6, 2, 0, 256)
+            q_h(5, 0, 256)
+            fin(3, 1, 1, 0, 256)
+            s2("A", 7, 0, 128)
+            s2("A", 7, 128, 256)
+            q_h(7, 0, 128)
+            mm2(7, 3, 0, 128)
+            fin(6, 2, 2, 0, 256)
+            q_h(7, 128, 256)
+            mm2(7, 0, 128, 256)
+            fin(7, 3, 3, 0, 128)
+            fin(7, 0, 4, 128, 256)

@@ -34,7 +34,7 @@ def tile_rows_gmlp_relu2_bias_res_kernel(tc, x, w1, hs, w2, b, r, out):
         x_bf = tiles("x_bf", 2, [P, NH, 4], BF16)
         x_q = tiles("x_q", 2, [P, NH], U32)
         x_s = tiles("x_s", 2, [P, NH], U8)
-        w1_raw = tiles("w1_raw", 4, [P, 4, 256], F32)
+        w1_raw = tiles("w1_raw", 2, [P, 4, 512], F32)
         w1_bf = tiles("w1_bf", 2, [P, 4, P, 4], BF16)
         w1_q = tiles("w1_q", 2, [P, 512], U32)
         w1_s = tiles("w1_s", 2, [P, 512], U8)
@@ -42,7 +42,7 @@ def tile_rows_gmlp_relu2_bias_res_kernel(tc, x, w1, hs, w2, b, r, out):
         w2_bf = tiles("w2_bf", 2, [P, 2, M, 4], BF16)
         w2_q = tiles("w2_q", 2, [P, 2 * M], U32)
         w2_s = tiles("w2_s", 2, [P, 2 * M], U8)
-        r_sb = tiles("r_sb", 2, [P, 4, NH], F32)
+        r_sb = tiles("r_sb", 2, [P, 2, N], F32)
         t_sb = tiles("t_sb", 8, [P, 4, NH], F32)
         h_bf = tiles("h_bf", 8, [P, NH, 4], BF16)
         h_q = tiles("h_q", 8, [P, NH], U32)
@@ -60,10 +60,10 @@ def tile_rows_gmlp_relu2_bias_res_kernel(tc, x, w1, hs, w2, b, r, out):
             nc.vector.quantize_mx(out=codes.bitcast(FP8X4), scales=scales, in_=values)
 
         def rows4(t, lo, hi):
-            return t[:, :, lo:hi].rearrange("p j (c i) -> p c j i", i=4)
+            return t[:, :, lo:hi].rearrange("p j (c i) -> p c j i", i=2)
 
         def words(t, lo, hi):
-            return t[:, lo:hi, :].rearrange("p (c i) j -> p c j i", i=4)
+            return t[:, lo:hi, :].rearrange("p (c i) j -> p c j i", i=2)
 
         def copy(eng, o, i):
             if eng == "A":
@@ -78,13 +78,13 @@ def tile_rows_gmlp_relu2_bias_res_kernel(tc, x, w1, hs, w2, b, r, out):
             nc.sync.dma_start(out=x_raw[h][:], in_=xv[:, :, h * NH:(h + 1) * NH])
 
         def load_w1(a):
-            nc.sync.dma_start(out=w1_raw[a][:], in_=w1v[:, :, a * 256:(a + 1) * 256])
+            nc.sync.dma_start(out=w1_raw[a][:], in_=w1v[:, :, a * 512:(a + 1) * 512])
 
         def load_w2(g, c):
             nc.sync.dma_start(out=w2_raw[2 * g + c][:], in_=w2[g, c * 512:(c + 1) * 512, :].rearrange("(p j) m -> p j m", j=4))
 
-        def load_r(h):
-            nc.sync.dma_start(out=r_sb[h][:], in_=r[:, :, h * NH:(h + 1) * NH].rearrange("g (t p) n -> p (g t) n", p=P))
+        def load_r(g):
+            nc.sync.dma_start(out=r_sb[g][:], in_=r[g].rearrange("(t p) n -> p t n", p=P))
 
         def i_x(eng, h, lo, hi):
             copy(eng, words(x_bf[h], lo, hi), rows4(x_raw[h], lo, hi))
@@ -92,17 +92,21 @@ def tile_rows_gmlp_relu2_bias_res_kernel(tc, x, w1, hs, w2, b, r, out):
         def q_x(h, lo, hi):
             quantize(x_q[h][:, lo:hi], x_s[h][:, lo:hi], x_bf[h][:, lo:hi, :].rearrange("p n j -> p (n j)"))
 
-        def i_w1(eng, a, lo, hi):
-            c, base = a // 2, (a % 2) * 64
-            copy(eng, w1_bf[c][:, :, base + lo:base + hi, :].rearrange("p t m j -> p m j t"),
-                 w1_raw[a][:, :, 4 * lo:4 * hi].rearrange("p j (m t) -> p m j t", t=4))
+        def i_w1(eng, c, lo, hi):
+            dst = w1_bf[c][:, :, lo:hi, :].rearrange("p (u t) m j -> p u m j t", t=2)
+            src = w1_raw[c][:, :, 4 * lo:4 * hi].rearrange("p j (m u t) -> p u m j t", u=2, t=2)
+            if eng == "A":
+                for u in range(2):
+                    nc.scalar.copy(out=dst[:, u], in_=src[:, u])
+            else:
+                nc.vector.tensor_copy(out=dst, in_=src)
 
         def q_w1(c, t0, t1):
             quantize(w1_q[c][:, t0 * P:t1 * P], w1_s[c][:, t0 * P:t1 * P],
                      w1_bf[c][:, t0:t1].rearrange("p t m j -> p (t m j)"))
 
         def i_w2(g, c):
-            sign = sgn[:, 2 * g + c, 0:4].unsqueeze(1).unsqueeze(3).to_broadcast([P, M // 4, 4, 4])
+            sign = sgn[:, 2 * g + c, 0:4].unsqueeze(1).unsqueeze(3).to_broadcast([P, M // 2, 4, 2])
             nc.vector.tensor_tensor(out=words(w2_bf[g][:, c], 0, M), in0=rows4(w2_raw[2 * g + c], 0, M), in1=sign, op=ALU.mult)
 
         def q_w2(g):
@@ -149,20 +153,18 @@ def tile_rows_gmlp_relu2_bias_res_kernel(tc, x, w1, hs, w2, b, r, out):
         def fin(u, bank, slot, lo, hi):
             c, g, h = UNITS[u]
             cols = slice(h * NH + lo, h * NH + hi)
-            nc.vector.tensor_tensor(out=y_sb[slot][:, :, lo:hi], in0=y_ps[bank][:, :, lo:hi], in1=r_sb[h][:, 2 * g:2 * g + 2, lo:hi], op=ALU.add)
+            nc.vector.tensor_tensor(out=y_sb[slot][:, :, lo:hi], in0=y_ps[bank][:, :, lo:hi], in1=r_sb[g][:, :, cols], op=ALU.add)
             nc.sync.dma_start(out=out[g, :, cols].rearrange("(t p) n -> p t n", p=P), in_=y_sb[slot][:, :, lo:hi])
 
         with tc.manual_schedule():
             nc.scalar.dma_start(out=live(hs_sb), in_=hs.rearrange("g (c p j) o -> p (g c) (j o)", p=P, j=4))
             nc.scalar.dma_start(out=live(b_sb), in_=b.rearrange("g (c p j) o -> p (g c) (j o)", p=P, j=4))
             load_w1(0)
-            load_w1(1)
             load_x(0)
-            load_w1(2)
-            load_w1(3)
+            load_w1(1)
+            load_x(1)
             load_w2(0, 0)
             load_w2(0, 1)
-            load_x(1)
             load_w2(1, 0)
             load_w2(1, 1)
             load_r(0)
@@ -175,15 +177,14 @@ def tile_rows_gmlp_relu2_bias_res_kernel(tc, x, w1, hs, w2, b, r, out):
             nc.vector.tensor_scalar(out=live(sgn), in0=live(two), scalar1=-1.0, scalar2=None, op0=ALU.add)
             nc.vector.reciprocal(out=live(inv), in_=live(half))
             i_w1("V", 0, 0, 40)
-            i_w1("A", 0, 40, 64)
+            i_w1("A", 0, 80, 128)
             nc.vector.scalar_tensor_tensor(out=live(quo), in0=live(mag), scalar=0.25, in1=live(inv), op0=ALU.mult, op1=ALU.mult)
-            i_w1("V", 1, 0, 40)
-            i_w1("A", 1, 40, 64)
+            i_w1("V", 0, 40, 80)
             nc.vector.tensor_tensor(out=live(root), in0=live(quo), in1=live(half), op=ALU.add)
             q_w1(0, 0, 2)
-            nc.vector.tensor_tensor(out=live(rootb), in0=live(root), in1=live(b_sb), op=ALU.mult)
             i_x("V", 0, 0, 128)
             i_x("A", 0, 128, 256)
+            nc.vector.tensor_tensor(out=live(rootb), in0=live(root), in1=live(b_sb), op=ALU.mult)
             q_w1(0, 2, 4)
             q_x(0, 0, 128)
             q_x(0, 128, 256)
@@ -191,73 +192,73 @@ def tile_rows_gmlp_relu2_bias_res_kernel(tc, x, w1, hs, w2, b, r, out):
             mm1(0, 1)
             mm1(1, 0)
             mm1(1, 1)
-            i_w1("V", 2, 0, 64)
             s1(0, 0)
             s1(0, 1)
-            i_w1("V", 3, 0, 64)
+            i_w1("V", 1, 0, 128)
             s1(1, 0)
             s1(1, 1)
-            s2("V", 0, 0, 128)
-            q_w1(1, 0, 4)
+            i_x("V", 1, 0, 128)
+            q_w1(1, 0, 2)
+            q_w1(1, 2, 4)
             mm1(2, 0)
             mm1(2, 1)
             mm1(3, 0)
             mm1(3, 1)
-            i_w2(0, 0)
-            s2("A", 0, 128, 256)
+            s2("A", 0, 0, 128)
+            s2("V", 0, 128, 256)
+            i_x("V", 1, 128, 256)
             s1(2, 0)
             s1(2, 1)
-            i_w2(0, 1)
-            s1(3, 0)
-            s1(3, 1)
-            i_x("V", 1, 0, 256)
-            q_h(0, 0, 256)
+            i_w2(0, 0)
             q_x(1, 0, 256)
             mm1(4, 0)
             mm1(4, 1)
+            s1(3, 0)
+            s1(3, 1)
             mm1(5, 0)
             mm1(5, 1)
-            q_w2(0)
+            s2("V", 1, 0, 256)
             s2("A", 2, 0, 256)
-            i_w2(1, 0)
-            s2("A", 3, 0, 128)
-            q_h(2, 0, 256)
-            mm2(2, 0, 0, 256)
+            i_w2(0, 1)
             s1(4, 0)
             s1(4, 1)
             mm1(6, 0)
             mm1(6, 1)
-            i_w2(1, 1)
-            s2("V", 1, 0, 256)
+            i_w2(1, 0)
+            q_w2(0)
             s1(5, 0)
             s1(5, 1)
             mm1(7, 0)
             mm1(7, 1)
-            q_w2(1)
-            s2("V", 3, 128, 256)
+            q_h(0, 0, 256)
+            q_h(2, 0, 256)
+            mm2(2, 0, 0, 256)
+            i_w2(1, 1)
+            s2("A", 3, 0, 256)
             q_h(1, 0, 256)
             s1(6, 0)
             s1(6, 1)
+            q_w2(1)
             q_h(3, 0, 256)
             mm2(3, 1, 0, 256)
             s2("A", 4, 0, 128)
             s2("V", 4, 128, 256)
-            fin(2, 0, 0, 0, 256)
-            s2("A", 6, 0, 256)
-            q_h(4, 0, 256)
-            s2("V", 5, 0, 256)
             s1(7, 0)
             s1(7, 1)
+            s2("V", 6, 0, 256)
+            q_h(4, 0, 256)
+            fin(2, 0, 0, 0, 256)
             q_h(6, 0, 256)
             mm2(6, 2, 0, 256)
-            q_h(5, 0, 256)
+            s2("A", 5, 0, 256)
             fin(3, 1, 1, 0, 256)
+            q_h(5, 0, 256)
             s2("A", 7, 0, 128)
             s2("A", 7, 128, 256)
             q_h(7, 0, 128)
             mm2(7, 3, 0, 128)
-            fin(6, 2, 2, 0, 256)
             q_h(7, 128, 256)
             mm2(7, 0, 128, 256)
+            fin(6, 2, 2, 0, 256)
             fin(7, 3, 3, 0, 128)
             fin(7, 0, 4, 128, 256)

from contextlib import ExitStack

import concourse.mybir as mybir

G, D, K, M, N = 2, 256, 1024, 256, 512
FLOPS = 2 * G * D * K * N + 2 * G * K * M * N

F32 = mybir.dt.float32
BF16 = mybir.dt.bfloat16
U32 = mybir.dt.uint32
U8 = mybir.dt.uint8
FP8X4 = mybir.dt.float8_e4m3fn_x4
ALU = mybir.AluOpType
ACT = mybir.ActivationFunctionType

P = 128
ROWS = 64
NH = 256
NC = 128
TINY = 2.0 ** -110
UNITS = [(0, 0, 0),(0, 1, 0),(1, 0, 0),(1, 1, 0),(0, 0, 1),(0, 1, 1),(1, 0, 1),(1, 1, 1)]


def tile_rows_gmlp_relu2_bias_res_kernel(tc, x, w1, hs, w2, b, r, out):
    nc = tc.nc
    with ExitStack() as ctx:
        sb = ctx.enter_context(tc.tile_pool(name="sb", bufs=1))
        ps = ctx.enter_context(tc.psum_pool(name="ps", bufs=1))

        def tiles(name, count, shape, dtype):
            return [sb.tile(shape, dtype, name="%s%d" % (name, i), align_bytes=64) for i in range(count)]

        x_raw = tiles("x_raw", 2, [P, 4, NH], F32)
        x_bf = tiles("x_bf", 2, [P, NH, 4], BF16)
        x_q = tiles("x_q", 2, [P, NH], U32)
        x_s = tiles("x_s", 2, [P, NH], U8)
        w1_raw = tiles("w1_raw", 2, [P, 4, 512], F32)
        w1_bf = tiles("w1_bf", 2, [P, 4, P, 4], BF16)
        w1_q = tiles("w1_q", 2, [P, 512], U32)
        w1_s = tiles("w1_s", 2, [P, 512], U8)
        w2_raw = tiles("w2_raw", 4, [P, 4, M], F32)
        w2_bf = tiles("w2_bf", 2, [P, 2, M, 4], BF16)
        w2_q = tiles("w2_q", 2, [P, 2 * M], U32)
        w2_s = tiles("w2_s", 2, [P, 2 * M], U8)
        r_sb = tiles("r_sb", 2, [P, 2, N], F32)
        t_sb = tiles("t_sb", 8, [P, 4, NH], F32)
        h_bf = tiles("h_bf", 8, [P, NH, 4], BF16)
        h_q = tiles("h_q", 8, [P, NH], U32)
        h_s = tiles("h_s", 8, [P, NH], U8)
        y_sb = tiles("y_sb", 5, [P, 2, NH], F32)
        hs_sb, b_sb, mag, half, inv, quo, root, rootb, two, sgn = tiles("small", 10, [P, 4, 8], F32)
        warm = tiles("warm", 2, [P, 1], F32)
        z_ps = [[ps.tile([P, 2, NH], F32, name="z%d%d" % (g, i)) for i in range(2)] for g in range(G)]
        y_ps = [ps.tile([P, 2, NH], F32, name="y%d" % i) for i in range(4)]

        def live(t):
            return t[:, :, 0:4]

        def quantize(codes, scales, values):
            nc.vector.quantize_mx(out=codes.bitcast(FP8X4), scales=scales, in_=values)

        def rows4(t, lo, hi):
            return t[:, :, lo:hi].rearrange("p j (c i) -> p c j i", i=2)

        def words(t, lo, hi):
            return t[:, lo:hi, :].rearrange("p (c i) j -> p c j i", i=2)

        def copy(eng, o, i):
            if eng == "A":
                nc.scalar.copy(out=o, in_=i)
            else:
                nc.vector.tensor_copy(out=o, in_=i)

        xv = x.rearrange("g (p j) n -> (g p) j n", j=4)
        w1v = w1.rearrange("g (p j) k -> (g p) j k", j=4)

        def load_x(h):
            nc.sync.dma_start(out=x_raw[h][:], in_=xv[:, :, h * NH:(h + 1) * NH])

        def load_w1(a):
            nc.sync.dma_start(out=w1_raw[a][:], in_=w1v[:, :, a * 512:(a + 1) * 512])

        def load_w2(g, c):
            nc.sync.dma_start(out=w2_raw[2 * g + c][:], in_=w2[g, c * 512:(c + 1) * 512, :].rearrange("(p j) m -> p j m", j=4))

        def load_r(g):
            nc.sync.dma_start(out=r_sb[g][:], in_=r[g].rearrange("(t p) n -> p t n", p=P))

        def i_x(eng, h, lo, hi):
            copy(eng, words(x_bf[h], lo, hi), rows4(x_raw[h], lo, hi))

        def q_x(h, lo, hi):
            quantize(x_q[h][:, lo:hi], x_s[h][:, lo:hi], x_bf[h][:, lo:hi, :].rearrange("p n j -> p (n j)"))

        def i_w1(eng, c, lo, hi):
            dst = w1_bf[c][:, :, lo:hi, :].rearrange("p (u t) m j -> p u m j t", t=2)
            src = w1_raw[c][:, :, 4 * lo:4 * hi].rearrange("p j (m u t) -> p u m j t", u=2, t=2)
            if eng == "A":
                for u in range(2):
                    nc.scalar.copy(out=dst[:, u], in_=src[:, u])
            else:
                nc.vector.tensor_copy(out=dst, in_=src)

        def q_w1(c, t0, t1):
            quantize(w1_q[c][:, t0 * P:t1 * P], w1_s[c][:, t0 * P:t1 * P],
                     w1_bf[c][:, t0:t1].rearrange("p t m j -> p (t m j)"))

        def i_w2(g, c):
            sign = sgn[:, 2 * g + c, 0:4].unsqueeze(1).unsqueeze(3).to_broadcast([P, M // 2, 4, 2])
            nc.vector.tensor_tensor(out=words(w2_bf[g][:, c], 0, M), in0=rows4(w2_raw[2 * g + c], 0, M), in1=sign, op=ALU.mult)

        def q_w2(g):
            quantize(w2_q[g][:], w2_s[g][:], w2_bf[g][:].rearrange("p c m j -> p (c m j)"))

        def mm1(u, i):
            c, g, h = UNITS[u]
            rows = slice(g * ROWS, (g + 1) * ROWS)
            for q in range(2):
                xc = slice(q * NC, (q + 1) * NC)
                for tt in range(2):
                    wc = slice((2 * i + tt) * P, (2 * i + tt + 1) * P)
                    nc.tensor.matmul_mx(out=z_ps[g][i][:, tt, xc], lhsT=w1_q[c][rows, wc].bitcast(FP8X4), lhsT_scale=w1_s[c][rows, wc],
                                        rhs=x_q[h][rows, xc].bitcast(FP8X4), rhs_scale=x_s[h][rows, xc], start=True, stop=True)

        def s1(u, i):
            c, g, h = UNITS[u]
            for tt in range(2):
                t = 2 * i + tt
                nc.scalar.activation(out=t_sb[u][:, t, :], in_=z_ps[g][i][:, tt, :], func=ACT.Relu,
                                     bias=rootb[:, 2 * g + c, t:t + 1], scale=root[:, 2 * g + c, t:t + 1])

        def s2(eng, u, lo, hi):
            src = rows4(t_sb[u], lo, hi)
            if eng == "A":
                nc.scalar.activation(out=words(h_bf[u], lo, hi), in_=src, func=ACT.Square)
            else:
                nc.vector.tensor_tensor(out=words(h_bf[u], lo, hi), in0=src, in1=src, op=ALU.mult)

        def q_h(u, lo, hi):
            quantize(h_q[u][:, lo:hi], h_s[u][:, lo:hi], h_bf[u][:, lo:hi, :].rearrange("p n j -> p (n j)"))

        def mm2(u, bank, lo, hi):
            g, h = UNITS[u][1:]
            for n0 in range(lo, hi, NC):
                xc = slice(n0, n0 + NC)
                for mt in range(2):
                    for c in range(2):
                        hu = UNITS.index((c, g, h))
                        wc = slice(c * M + mt * P, c * M + (mt + 1) * P)
                        nc.tensor.matmul_mx(out=y_ps[bank][:, mt, xc], lhsT=w2_q[g][:, wc].bitcast(FP8X4), lhsT_scale=w2_s[g][:, wc],
                                            rhs=h_q[hu][:, xc].bitcast(FP8X4), rhs_scale=h_s[hu][:, xc], start=(c == 0), stop=(c == 1))

        def fin(u, bank, slot, lo, hi):
            c, g, h = UNITS[u]
            cols = slice(h * NH + lo, h * NH + hi)
            nc.vector.tensor_tensor(out=y_sb[slot][:, :, lo:hi], in0=y_ps[bank][:, :, lo:hi], in1=r_sb[g][:, :, cols], op=ALU.add)
            nc.sync.dma_start(out=out[g, :, cols].rearrange("(t p) n -> p t n", p=P), in_=y_sb[slot][:, :, lo:hi])

        with tc.manual_schedule():
            nc.scalar.dma_start(out=live(hs_sb), in_=hs.rearrange("g (c p j) o -> p (g c) (j o)", p=P, j=4))
            nc.scalar.dma_start(out=live(b_sb), in_=b.rearrange("g (c p j) o -> p (g c) (j o)", p=P, j=4))
            load_w1(0)
            load_x(0)
            load_w1(1)
            load_x(1)
            load_w2(0, 0)
            load_w2(0, 1)
            load_w2(1, 0)
            load_w2(1, 1)
            load_r(0)
            load_r(1)
            nc.vector.memset(warm[0][:], 1.0)
            nc.scalar.activation(out=warm[1][:], in_=warm[0][:], func=ACT.Sqrt)
            nc.vector.scalar_tensor_tensor(out=live(mag), in0=live(hs_sb), scalar=-1.0, in1=live(hs_sb), op0=ALU.mult, op1=ALU.max)
            nc.vector.tensor_scalar(out=live(two), in0=live(hs_sb), scalar1=0.0, scalar2=2.0, op0=ALU.is_ge, op1=ALU.mult)
            nc.scalar.activation(out=live(half), in_=live(mag), func=ACT.Sqrt, scale=0.25, bias=TINY)
            nc.vector.tensor_scalar(out=live(sgn), in0=live(two), scalar1=-1.0, scalar2=None, op0=ALU.add)
            nc.vector.reciprocal(out=live(inv), in_=live(half))
            i_w1("V", 0, 0, 40)
            i_w1("A", 0, 80, 128)
            nc.vector.scalar_tensor_tensor(out=live(quo), in0=live(mag), scalar=0.25, in1=live(inv), op0=ALU.mult, op1=ALU.mult)
            i_w1("V", 0, 40, 80)
            nc.vector.tensor_tensor(out=live(root), in0=live(quo), in1=live(half), op=ALU.add)
            q_w1(0, 0, 2)
            i_x("V", 0, 0, 128)
            i_x("A", 0, 128, 256)
            nc.vector.tensor_tensor(out=live(rootb), in0=live(root), in1=live(b_sb), op=ALU.mult)
            q_w1(0, 2, 4)
            q_x(0, 0, 128)
            q_x(0, 128, 256)
            mm1(0, 0)
            mm1(0, 1)
            mm1(1, 0)
            mm1(1, 1)
            s1(0, 0)
            s1(0, 1)
            i_w1("V", 1, 0, 128)
            s1(1, 0)
            s1(1, 1)
            i_x("V", 1, 0, 128)
            q_w1(1, 0, 2)
            q_w1(1, 2, 4)
            mm1(2, 0)
            mm1(2, 1)
            mm1(3, 0)
            mm1(3, 1)
            s2("A", 0, 0, 128)
            s2("V", 0, 128, 256)
            i_x("V", 1, 128, 256)
            s1(2, 0)
            s1(2, 1)
            i_w2(0, 0)
            q_x(1, 0, 256)
            mm1(4, 0)
            mm1(4, 1)
            s1(3, 0)
            s1(3, 1)
            mm1(5, 0)
            mm1(5, 1)
            s2("V", 1, 0, 256)
            s2("A", 2, 0, 256)
            i_w2(0, 1)
            s1(4, 0)
            s1(4, 1)
            mm1(6, 0)
            mm1(6, 1)
            i_w2(1, 0)
            q_w2(0)
            s1(5, 0)
            s1(5, 1)
            mm1(7, 0)
            mm1(7, 1)
            q_h(0, 0, 256)
            q_h(2, 0, 256)
            mm2(2, 0, 0, 256)
            i_w2(1, 1)
            s2("A", 3, 0, 256)
            q_h(1, 0, 256)
            s1(6, 0)
            s1(6, 1)
            q_w2(1)
            q_h(3, 0, 256)
            mm2(3, 1, 0, 256)
            s2("A", 4, 0, 128)
            s2("V", 4, 128, 256)
            s1(7, 0)
            s1(7, 1)
            s2("V", 6, 0, 256)
            q_h(4, 0, 256)
            fin(2, 0, 0, 0, 256)
            q_h(6, 0, 256)
            mm2(6, 2, 0, 256)
            s2("A", 5, 0, 256)
            fin(3, 1, 1, 0, 256)
            q_h(5, 0, 256)
            s2("A", 7, 0, 128)
            s2("A", 7, 128, 256)
            q_h(7, 0, 128)
            mm2(7, 3, 0, 128)
            q_h(7, 128, 256)
            mm2(7, 0, 128, 256)
            fin(6, 2, 2, 0, 256)
            fin(7, 3, 3, 0, 128)
            fin(7, 0, 4, 128, 256)
